import numpy as np
import ml_dtypes


def mxq(x, axis, fmt="e4m3"):
    dtype, down = {"e4m3": (ml_dtypes.float8_e4m3fn, 7), "e5m2": (ml_dtypes.float8_e5m2, 14)}[fmt]
    v = np.moveaxis(np.asarray(x, np.float32).astype(ml_dtypes.bfloat16).astype(np.float64), axis, -1)
    blocks = v.reshape(v.shape[:-1] + (-1, 32))
    amax = np.abs(blocks).max(-1, keepdims=True)
    byte = np.maximum(np.where(amax > 0, np.frexp(amax)[1] - 1 + 127, 0) - down, 1)
    scale = np.exp2(byte - 127.0)
    codes = (blocks / scale).astype(np.float32).astype(dtype).astype(np.float64)
    return np.moveaxis((codes * scale).reshape(v.shape), -1, axis)


WIDE = False


def mx_kscale(k):
    if not WIDE:
        return np.ones(k)
    levels = np.array([30, -30])
    if k % 512:
        return np.exp2(np.random.permutation(np.resize(levels, k // 32))).repeat(32)
    a = np.empty((k // 512, 16))
    for p in range(k // 512):
        a[p, :8] = np.random.permutation(np.resize(levels, 8))
        for g in range(8):
            far = levels[np.abs(levels - a[p, g]) >= 10]
            a[p, g + 8] = far[np.random.randint(len(far))]
    return np.exp2(a.ravel()).repeat(32)


def f64(x):
    return np.asarray(x).astype(np.float64)


def striped(idx):
    return np.tile(np.asarray(idx).reshape(-1, 16).T, (8, 1)).astype(np.uint16)


def unstriped(offs):
    return offs[:16].T.reshape(-1).astype(np.int64)


E2M1 = np.array([0.0, 0.5, 1.0, 1.5, 2.0, 3.0, 4.0, 6.0, -0.0, -0.5, -1.0, -1.5, -2.0, -3.0, -4.0, -6.0])


def pack_weight(w, fmt):
    k, n = w.shape
    w = f64(np.asarray(w, np.float32).astype(ml_dtypes.bfloat16)).reshape(k // 32, 32, n)
    amax = np.abs(w).max(1)
    if fmt in ("e4m3", "e5m2"):
        byte = np.frexp(amax)[1] - 1 + 127 - (7 if fmt == "e4m3" else 14)
    else:
        mant, ex = np.frexp(amax / 6.0)
        byte = np.where(mant > 0.5, ex, ex - 1) + 127
    byte = np.clip(np.where(amax > 0, byte, 1), 1, 254)
    scaled = (w * np.exp2(127.0 - byte)[:, None, :]).reshape(k, n).astype(np.float32)
    by_word = np.ascontiguousarray(scaled.reshape(k // 512, 128, 4, n).transpose(0, 1, 3, 2))
    if fmt in ("e4m3", "e5m2"):
        words = by_word.astype(ml_dtypes.float8_e4m3fn if fmt == "e4m3" else ml_dtypes.float8_e5m2).view(np.uint8)
    else:
        c = by_word.astype(ml_dtypes.float4_e2m1fn).view(np.uint8) & 0xF
        words = (c[..., 0::2] | (c[..., 1::2] << 4)).reshape(k // 512, 128, 2 * n)
    return np.ascontiguousarray(words), np.ascontiguousarray(byte.astype(np.uint8).reshape(k // 512, 16, n))


def unpack_weight(words, scales, fmt):
    g, _, n = scales.shape
    words = np.ascontiguousarray(words).reshape(g, 128, n, -1)
    if fmt in ("e4m3", "e5m2"):
        vals = words.view(ml_dtypes.float8_e4m3fn if fmt == "e4m3" else ml_dtypes.float8_e5m2).astype(np.float64)
    else:
        nib = np.empty((g, 128, n, 4), np.uint8)
        nib[..., 0::2] = words & 0xF
        nib[..., 1::2] = words >> 4
        vals = E2M1[nib]
    vals = vals * np.repeat(np.exp2(scales.astype(np.float64) - 127.0), 8, axis=1)[..., None]
    return vals.transpose(0, 1, 3, 2).reshape(g * 512, n)


def sigmoid(v):
    return 1.0 / (1.0 + np.exp(-v))


def sgn(shape):
    return np.random.uniform(0.5, 2.0, shape) * np.where(np.random.standard_normal(shape) < 0, -1.0, 1.0)


K, T, J, R, F, Z, O, U, D, N = 512, 1024, 256, 512, 512, 1024, 128, 128, 256, 256


def setup_inputs():
    n = np.random.standard_normal
    idx = np.random.permutation(T)[:J]
    idx2 = np.random.permutation(Z)[:J]
    idx3 = np.random.permutation(J)[:O]
    idx4 = np.random.permutation(J)[:O]
    idx5 = np.random.permutation(J)[:U]
    idx6 = np.random.permutation(J)[:U]
    idx7 = np.random.permutation(T)[:D]
    fk = mx_kscale(K)
    ff = mx_kscale(F)
    fr = mx_kscale(R)
    xtp = pack_weight(n((K, T)) / fk[:, None], "e4m3")
    xop = pack_weight(n((F, Z)) / ff[:, None], "e2m1")
    wp = pack_weight(n((K, R)) * 1 / np.sqrt(K) * fk[:, None], "e2m1")
    w2p = pack_weight(n((F, R)) * 1 / np.sqrt(F) * ff[:, None], "e5m2")
    wbp = pack_weight(n((R, N)) * 1 / np.sqrt(R) / fr[:, None], "e5m2")
    wsp = pack_weight(n((K, N)) * 1 / np.sqrt(K) * fk[:, None], "e5m2")
    return {
        "xt_words": xtp[0],
        "xt_scales": xtp[1],
        "xo_words": xop[0],
        "xo_scales": xop[1],
        "w_words": wp[0],
        "w_scales": wp[1],
        "w2_words": w2p[0],
        "w2_scales": w2p[1],
        "sa": (np.random.uniform(0.5, 1.6, (R, 1)) * fr[:, None]).astype(np.float32),
        "sb": (np.random.uniform(0.5, 1.6, (R, 1)) * fr[:, None]).astype(np.float32),
        "sg": (sgn((R, 1))).astype(np.float32),
        "bg": (np.random.uniform(-2.0, 2.0, (R, 1))).astype(np.float32),
        "sh": (sgn((R, 1))).astype(np.float32),
        "bh": (np.random.uniform(-2.0, 2.0, (R, 1))).astype(np.float32),
        "wb_words": wbp[0],
        "wb_scales": wbp[1],
        "ws_words": wsp[0],
        "ws_scales": wsp[1],
        "offs": striped(idx),
        "offs2": striped(idx2),
        "offs3": striped(idx3),
        "offs4": striped(idx4),
        "offs5": striped(idx5),
        "offs6": striped(idx6),
        "offs7": striped(idx7),
    }


def reference(xt_words, xt_scales, xo_words, xo_scales, w_words, w_scales, w2_words, w2_scales, sa, sb, sg, bg, sh, bh, wb_words, wb_scales, ws_words, ws_scales, offs, offs2, offs3, offs4, offs5, offs6, offs7):
    idx = unstriped(offs)
    idx2 = unstriped(offs2)
    idx3 = unstriped(offs3)
    idx4 = unstriped(offs4)
    idx5 = unstriped(offs5)
    idx6 = unstriped(offs6)
    idx7 = unstriped(offs7)
    xtu = unpack_weight(xt_words, xt_scales, "e4m3")
    xou = unpack_weight(xo_words, xo_scales, "e2m1")
    wu = unpack_weight(w_words, w_scales, "e2m1")
    w2u = unpack_weight(w2_words, w2_scales, "e5m2")
    wbu = unpack_weight(wb_words, wb_scales, "e5m2")
    wsu = unpack_weight(ws_words, ws_scales, "e5m2")
    xtidxg = xtu[:, idx]
    a = wu.T @ xtidxg
    xoidx2g = xou[:, idx2]
    b = w2u.T @ xoidx2g
    h1 = a[:, idx3] * f64(sa) * sigmoid(a[:, idx4] * f64(sg) + f64(bg))
    h2 = b[:, idx5] * f64(sb) * sigmoid(b[:, idx6] * f64(sh) + f64(bh))
    hid = np.concatenate([h1, h2], axis=1)
    hidq = mxq(hid, 0, "e4m3")
    xtidx7g = xtu[:, idx7]
    y = wbu.T @ hidq + wsu.T @ xtidx7g
    return y

@@ -1,0 +1,209 @@
+from contextlib import ExitStack
+
+import concourse.mybir as mybir
+
+K, T, J, R, Z, O, D, N = 512, 1024, 256, 512, 1024, 128, 256, 256
+FLOPS = 2 * (K * R * J + K * R * J + R * N * D + K * N * D)
+
+F32 = mybir.dt.float32
+BF16 = mybir.dt.bfloat16
+I32 = mybir.dt.int32
+U32 = mybir.dt.uint32
+U16 = mybir.dt.uint16
+U8 = mybir.dt.uint8
+E4M3 = mybir.dt.float8_e4m3fn_x4
+E5M2 = mybir.dt.float8_e5m2_x4
+E2M1 = mybir.dt.float4_e2m1fn_x4
+ACT = mybir.ActivationFunctionType
+MULT = mybir.AluOpType.mult
+
+P = 128
+PACK = 4
+QUADS = 4
+QUAD = 32
+
+
+def tile_list_gatedsides_twotab_further_plain_kernel(
+    tc, xt_words, xt_scales, xo_words, xo_scales, w_words, w_scales, w2_words, w2_scales,
+    sa, sb, sg, bg, sh, bh, wb_words, wb_scales, ws_words, ws_scales,
+    offs, offs2, offs3, offs4, offs5, offs6, offs7, out,
+):
+    nc = tc.nc
+    with ExitStack() as ctx:
+        keep = ctx.enter_context(tc.tile_pool(name="keep", bufs=1))
+        psum = ctx.enter_context(tc.psum_pool(name="psum", bufs=1))
+
+        def tile(shape, dtype, name, tag=None):
+            return keep.tile(shape, dtype, name=name, tag=tag or name, align_bytes=64)
+
+        def load_list(src, name):
+            t = tile(list(src.shape), U16, name)
+            nc.sync.dma_start(t[:], src)
+            return t
+
+        def load_words(src, cols, dtype, name):
+            t = tile([P, cols], dtype, name)
+            nc.sync.dma_start(t[:].bitcast(I32), src.bitcast(I32))
+            return t
+
+        def load_scale_rows(src, name):
+            cols = src.shape[2]
+            t = tile([PACK, QUADS, cols // 4], I32, name)
+            nc.sync.dma_start(t[:], src[0].rearrange("(q r) n -> r q n", r=PACK).bitcast(I32))
+            return t
+
+        def load_column(src, name):
+            t = tile([P, PACK], F32, name)
+            nc.sync.dma_start(t[:], src.rearrange("(p t) o -> p (t o)", t=PACK))
+            return t
+
+        def zeroed_plane(cols, name):
+            t = tile([P, cols], U8, name)
+            nc.vector.memset(t[:].bitcast(I32), 0)
+            return t
+
+        def load_plane(plane, src):
+            for q in range(QUADS):
+                nc.sync.dma_start(
+                    plane[QUAD * q : QUAD * q + PACK, :].bitcast(I32), src[0, PACK * q : PACK * (q + 1), :].bitcast(I32)
+                )
+
+        def spread(plane, rows):
+            for q in range(QUADS):
+                nc.vector.tensor_copy(plane[QUAD * q : QUAD * q + PACK, :].bitcast(I32), rows[:, q, :])
+
+        def gather(window, offsets, dtype, name, tag=None):
+            t = tile([P, 16 * offsets.shape[1]], dtype, name, tag)
+            nc.vector.tensor_copy(t[:], window[:].indirect(offsets[:]))
+            return t
+
+        def deal(copy, src, dtype, name):
+            t = tile([P, R], dtype, name)
+            copy(t[:].rearrange("p (t m) -> p m t", t=PACK), src[:].rearrange("p (m t) -> p m t", t=PACK))
+            return t
+
+        def fp8_words(src):
+            return src[0].rearrange("p n t -> p (n t)")
+
+        xo_s = zeroed_plane(Z, "xo_s")
+        w2_s = zeroed_plane(R, "w2_s")
+        xt_s = zeroed_plane(T, "xt_s")
+        w_s = zeroed_plane(R, "w_s")
+        ws_s = zeroed_plane(N, "ws_s")
+        wb_s = zeroed_plane(N, "wb_s")
+
+        w2_rows = load_scale_rows(w2_scales, "w2_rows")
+        list2 = load_list(offs2, "list2")
+        xo_w = load_words(xo_words[0], Z, U16, "xo_w")
+        load_plane(xo_s, xo_scales)
+        w2_w = load_words(fp8_words(w2_words), R, U32, "w2_w")
+        w_w = load_words(w_words[0], R, U16, "w_w")
+        xt_w = load_words(fp8_words(xt_words), T, U32, "xt_w")
+        list6 = load_list(offs6, "list6")
+        sh_c = load_column(sh, "sh_c")
+        bh_c = load_column(bh, "bh_c")
+        list5 = load_list(offs5, "list5")
+        sb_c = load_column(sb, "sb_c")
+        list1 = load_list(offs, "list1")
+        load_plane(xt_s, xt_scales)
+        load_plane(w_s, w_scales)
+        list4 = load_list(offs4, "list4")
+        sg_c = load_column(sg, "sg_c")
+        bg_c = load_column(bg, "bg_c")
+        list3 = load_list(offs3, "list3")
+        sa_c = load_column(sa, "sa_c")
+        list7 = load_list(offs7, "list7")
+        ws_w = load_words(fp8_words(ws_words), N, U32, "ws_w")
+        wb_w = load_words(fp8_words(wb_words), N, U32, "wb_w")
+        load_plane(ws_s, ws_scales)
+        load_plane(wb_s, wb_scales)
+        def first_stage(side, bank0, lhs_w, lhs_s, lhs_fmt, rhs_w, rhs_s, rhs_fmt):
+            banks = []
+            for t in range(PACK):
+                cols = slice(t * P, (t + 1) * P)
+                acc = psum.tile([P, J], F32, name="%s_acc%d" % (side, t), tag="bank%d" % (bank0 + t))
+                nc.tensor.matmul_mx(
+                    out=acc[:], lhsT=lhs_w[:, cols].bitcast(lhs_fmt), lhsT_scale=lhs_s[:, cols],
+                    rhs=rhs_w[:].bitcast(rhs_fmt), rhs_scale=rhs_s[:], start=True, stop=True,
+                )
+                banks.append(acc)
+            return banks
+
+        def looks(side, banks, copiers, gate_list, slope, offset, value_list, weight):
+            gates = tile([P, PACK, O], F32, side + "_gates")
+            values = tile([P, PACK, O], F32, side + "_values")
+            for t in range(PACK):
+                rows = tile([P, J], F32, "%s_rows%d" % (side, t))
+                copiers[t](rows[:], banks[t][:])
+                nc.scalar.activation(
+                    out=gates[:, t, :], in_=rows[:].indirect(gate_list[:]), func=ACT.Sigmoid,
+                    bias=offset[:, t : t + 1], scale=slope[:, t : t + 1],
+                )
+                nc.scalar.activation(
+                    out=values[:, t, :], in_=rows[:].indirect(value_list[:]), func=ACT.Copy,
+                    scale=weight[:, t : t + 1],
+                )
+            return gates, values
+
+        def hidden(side, gates, values, tag=None):
+            hid = tile([P, O * PACK], BF16, side + "_hid", tag)
+            nc.vector.tensor_tensor(
+                hid[:].rearrange("p (c i t) -> p c t i", i=4, t=PACK),
+                values[:].rearrange("p t (c i) -> p c t i", i=4),
+                gates[:].rearrange("p t (c i) -> p c t i", i=4),
+                MULT,
+            )
+            codes = tile([P, O], U32, side + "_codes")
+            scales = tile([P, O], U8, side + "_scales")
+            nc.vector.quantize_mx(out=codes[:].bitcast(E4M3), scales=scales[:], in_=hid[:])
+            return codes, scales
+
+        def short_way(side, bank0, d0):
+            banks = []
+            for n in range(N // P):
+                cols = slice(n * P, (n + 1) * P)
+                acc = psum.tile([P, O], F32, name="%s_out%d" % (side, n), tag="bank%d" % (bank0 + n))
+                nc.tensor.matmul_mx(
+                    out=acc[:], lhsT=ws_w[:, cols].bitcast(E5M2), lhsT_scale=ws_s[:, cols],
+                    rhs=x7_w[:, d0 : d0 + O].bitcast(E4M3), rhs_scale=x7_s[:, d0 : d0 + O], start=True, stop=False,
+                )
+                banks.append(acc)
+            return banks
+
+        def finish(side, banks, codes, scales, d0, copiers, queues):
+            for n in range(N // P):
+                cols = slice(n * P, (n + 1) * P)
+                nc.tensor.matmul_mx(
+                    out=banks[n][:], lhsT=wb_w[:, cols].bitcast(E5M2), lhsT_scale=wb_s[:, cols],
+                    rhs=codes[:].bitcast(E4M3), rhs_scale=scales[:], start=False, stop=True,
+                )
+            for n in range(N // P):
+                res = tile([P, O], F32, "%s_res%d" % (side, n))
+                copiers[n](res[:], banks[n][:])
+                queues[n].dma_start(out[n * P : (n + 1) * P, d0 : d0 + O], res[:])
+
+        vcopy, scopy = nc.vector.tensor_copy, nc.scalar.copy
+
+        spread(w2_s, w2_rows)
+        xo_gw = gather(xo_w, list2, U16, "xo_gw")
+        w2_sd = deal(vcopy, w2_s, U8, "w2_sd")
+        xo_gs = gather(xo_s, list2, U8, "xo_gs")
+        w2_wd = deal(scopy, w2_w, U32, "w2_wd")
+        w_wd = deal(scopy, w_w, U16, "w_wd")
+        b_banks = first_stage("b", 0, w2_wd, w2_sd, E5M2, xo_gw, xo_gs, E2M1)
+
+        xt_gw = gather(xt_w, list1, U32, "xt_gw")
+        xt_gs = gather(xt_s, list1, U8, "xt_gs")
+        w_sd = deal(vcopy, w_s, U8, "w_sd")
+        b_gates, b_values = looks("b", b_banks, [scopy, vcopy, vcopy, vcopy], list6, sh_c, bh_c, list5, sb_c)
+        a_banks = first_stage("a", 4, w_wd, w_sd, E2M1, xt_gw, xt_gs, E4M3)
+        a_gates, a_values = looks("a", a_banks, [vcopy] * 4, list4, sg_c, bg_c, list3, sa_c)
+
+        b_codes, b_scales = hidden("b", b_gates, b_values, "w_wd")
+        x7_w = gather(xt_w, list7, U32, "x7_w", "xt_gw")
+        x7_s = gather(xt_s, list7, U8, "x7_s", "xt_gs")
+        b_out = short_way("b", 4, O)
+        finish("b", b_out, b_codes, b_scales, O, [vcopy, vcopy], [nc.sync, nc.sync])
+        a_out = short_way("a", 6, 0)
+        a_codes, a_scales = hidden("a", a_gates, a_values)
+        finish("a", a_out, a_codes, a_scales, 0, [vcopy, scopy], [nc.sync, nc.scalar])

@@ -41,20 +41,20 @@ def tile_list_gatedsides_twotab_further_plain_kernel(
             nc.sync.dma_start(t[:], src)
             return t
 
-        def load_words(src, cols, dtype, name):
+        def load_words(src, cols, dtype, name, queue=nc.sync):
             t = tile([P, cols], dtype, name)
-            nc.sync.dma_start(t[:].bitcast(I32), src.bitcast(I32))
+            queue.dma_start(t[:].bitcast(I32), src.bitcast(I32))
             return t
 
-        def load_scale_rows(src, name):
+        def load_scale_rows(src, name, queue=nc.sync):
             cols = src.shape[2]
             t = tile([PACK, QUADS, cols // 4], I32, name)
-            nc.sync.dma_start(t[:], src[0].rearrange("(q r) n -> r q n", r=PACK).bitcast(I32))
+            queue.dma_start(t[:], src[0].rearrange("(q r) n -> r q n", r=PACK).bitcast(I32))
             return t
 
-        def load_column(src, name):
+        def load_column(src, name, queue=nc.sync):
             t = tile([P, PACK], F32, name)
-            nc.sync.dma_start(t[:], src.rearrange("(p t) o -> p (t o)", t=PACK))
+            queue.dma_start(t[:], src.rearrange("(p t) o -> p (t o)", t=PACK))
             return t
 
         def zeroed_plane(cols, name):
@@ -82,31 +82,37 @@ def tile_list_gatedsides_twotab_further_plain_kernel(
             copy(t[:].rearrange("p (t m) -> p m t", t=PACK), src[:].rearrange("p (m t) -> p m t", t=PACK))
             return t
 
+        def deal_slots(dealt, src, t0, t1):
+            nc.vector.tensor_copy(
+                dealt[:].rearrange("p (t m) -> p m t", t=PACK)[:, :, t0:t1],
+                src[:].rearrange("p (m t) -> p m t", t=PACK)[:, :, t0:t1],
+            )
+
         def fp8_words(src):
             return src[0].rearrange("p n t -> p (n t)")
 
-        xo_s = zeroed_plane(Z, "xo_s")
-        w2_s = zeroed_plane(R, "w2_s")
         xt_s = zeroed_plane(T, "xt_s")
-        w_s = zeroed_plane(R, "w_s")
         ws_s = zeroed_plane(N, "ws_s")
         wb_s = zeroed_plane(N, "wb_s")
+        w2_s = zeroed_plane(R, "w2_s")
+        xo_s = zeroed_plane(Z, "xo_s")
+        w_s = zeroed_plane(R, "w_s")
 
+        xo_w = load_words(xo_words[0], Z, U16, "xo_w", nc.scalar)
+        w2_w = load_words(fp8_words(w2_words), R, U32, "w2_w", nc.scalar)
+        w_w = load_words(w_words[0], R, U16, "w_w", nc.scalar)
+        xt_w = load_words(fp8_words(xt_words), T, U32, "xt_w", nc.scalar)
         w2_rows = load_scale_rows(w2_scales, "w2_rows")
+        xo_rows = load_scale_rows(xo_scales, "xo_rows")
         list2 = load_list(offs2, "list2")
-        xo_w = load_words(xo_words[0], Z, U16, "xo_w")
-        load_plane(xo_s, xo_scales)
-        w2_w = load_words(fp8_words(w2_words), R, U32, "w2_w")
-        w_w = load_words(w_words[0], R, U16, "w_w")
-        xt_w = load_words(fp8_words(xt_words), T, U32, "xt_w")
+        w_rows = load_scale_rows(w_scales, "w_rows")
         list6 = load_list(offs6, "list6")
         sh_c = load_column(sh, "sh_c")
         bh_c = load_column(bh, "bh_c")
-        list5 = load_list(offs5, "list5")
-        sb_c = load_column(sb, "sb_c")
         list1 = load_list(offs, "list1")
         load_plane(xt_s, xt_scales)
-        load_plane(w_s, w_scales)
+        list5 = load_list(offs5, "list5")
+        sb_c = load_column(sb, "sb_c")
         list4 = load_list(offs4, "list4")
         sg_c = load_column(sg, "sg_c")
         bg_c = load_column(bg, "bg_c")
@@ -117,6 +123,11 @@ def tile_list_gatedsides_twotab_further_plain_kernel(
         wb_w = load_words(fp8_words(wb_words), N, U32, "wb_w")
         load_plane(ws_s, ws_scales)
         load_plane(wb_s, wb_scales)
+
+        warm_in = tile([P, 1], F32, "warm_in")
+        warm_out = tile([P, 1], F32, "warm_out")
+        nc.vector.memset(warm_in[:], 0.0)
+        nc.scalar.activation(out=warm_out[:], in_=warm_in[:], func=ACT.Sigmoid)
         def first_stage(side, bank0, lhs_w, lhs_s, lhs_fmt, rhs_w, rhs_s, rhs_fmt):
             banks = []
             for t in range(PACK):
@@ -170,7 +181,7 @@ def tile_list_gatedsides_twotab_further_plain_kernel(
                 banks.append(acc)
             return banks
 
-        def finish(side, banks, codes, scales, d0, copiers, queues):
+        def finish(side, banks, codes, scales, d0, copiers, queues, tags):
             for n in range(N // P):
                 cols = slice(n * P, (n + 1) * P)
                 nc.tensor.matmul_mx(
@@ -178,24 +189,29 @@ def tile_list_gatedsides_twotab_further_plain_kernel(
                     rhs=codes[:].bitcast(E4M3), rhs_scale=scales[:], start=False, stop=True,
                 )
             for n in range(N // P):
-                res = tile([P, O], F32, "%s_res%d" % (side, n))
+                res = tile([P, O], F32, "%s_res%d" % (side, n), tags[n])
                 copiers[n](res[:], banks[n][:])
                 queues[n].dma_start(out[n * P : (n + 1) * P, d0 : d0 + O], res[:])
 
         vcopy, scopy = nc.vector.tensor_copy, nc.scalar.copy
 
         spread(w2_s, w2_rows)
+        spread(xo_s, xo_rows)
+        w2_sd = tile([P, R], U8, "w2_sd")
+        deal_slots(w2_sd, w2_s, 0, 1)
         xo_gw = gather(xo_w, list2, U16, "xo_gw")
-        w2_sd = deal(vcopy, w2_s, U8, "w2_sd")
         xo_gs = gather(xo_s, list2, U8, "xo_gs")
+        deal_slots(w2_sd, w2_s, 1, PACK)
         w2_wd = deal(scopy, w2_w, U32, "w2_wd")
         w_wd = deal(scopy, w_w, U16, "w_wd")
         b_banks = first_stage("b", 0, w2_wd, w2_sd, E5M2, xo_gw, xo_gs, E2M1)
 
+        spread(w_s, w_rows)
+        w_sd = tile([P, R], U8, "w_sd")
+        deal_slots(w_sd, w_s, 0, PACK)
         xt_gw = gather(xt_w, list1, U32, "xt_gw")
         xt_gs = gather(xt_s, list1, U8, "xt_gs")
-        w_sd = deal(vcopy, w_s, U8, "w_sd")
-        b_gates, b_values = looks("b", b_banks, [scopy, vcopy, vcopy, vcopy], list6, sh_c, bh_c, list5, sb_c)
+        b_gates, b_values = looks("b", b_banks, [scopy, scopy, scopy, vcopy], list6, sh_c, bh_c, list5, sb_c)
         a_banks = first_stage("a", 4, w_wd, w_sd, E2M1, xt_gw, xt_gs, E4M3)
         a_gates, a_values = looks("a", a_banks, [vcopy] * 4, list4, sg_c, bg_c, list3, sa_c)
 
@@ -203,7 +219,7 @@ def tile_list_gatedsides_twotab_further_plain_kernel(
         x7_w = gather(xt_w, list7, U32, "x7_w", "xt_gw")
         x7_s = gather(xt_s, list7, U8, "x7_s", "xt_gs")
         b_out = short_way("b", 4, O)
-        finish("b", b_out, b_codes, b_scales, O, [vcopy, vcopy], [nc.sync, nc.sync])
+        finish("b", b_out, b_codes, b_scales, O, [scopy, scopy], [nc.sync, nc.sync], ["a_rows2", "a_rows3"])
         a_out = short_way("a", 6, 0)
         a_codes, a_scales = hidden("a", a_gates, a_values)
-        finish("a", a_out, a_codes, a_scales, 0, [vcopy, scopy], [nc.sync, nc.scalar])
+        finish("a", a_out, a_codes, a_scales, 0, [vcopy, scopy], [nc.sync, nc.scalar], [None, None])

@@ -41,20 +41,20 @@ def tile_list_gatedsides_twotab_further_plain_kernel(
             nc.sync.dma_start(t[:], src)
             return t
 
-        def load_words(src, cols, dtype, name, queue=nc.sync):
+        def load_words(src, cols, dtype, name):
             t = tile([P, cols], dtype, name)
-            queue.dma_start(t[:].bitcast(I32), src.bitcast(I32))
+            nc.sync.dma_start(t[:].bitcast(I32), src.bitcast(I32))
             return t
 
-        def load_scale_rows(src, name, queue=nc.sync):
+        def load_scale_rows(src, name):
             cols = src.shape[2]
             t = tile([PACK, QUADS, cols // 4], I32, name)
-            queue.dma_start(t[:], src[0].rearrange("(q r) n -> r q n", r=PACK).bitcast(I32))
+            nc.sync.dma_start(t[:], src[0].rearrange("(q r) n -> r q n", r=PACK).bitcast(I32))
             return t
 
-        def load_column(src, name, queue=nc.sync):
+        def load_column(src, name):
             t = tile([P, PACK], F32, name)
-            queue.dma_start(t[:], src.rearrange("(p t) o -> p (t o)", t=PACK))
+            nc.sync.dma_start(t[:], src.rearrange("(p t) o -> p (t o)", t=PACK))
             return t
 
         def zeroed_plane(cols, name):
@@ -82,37 +82,31 @@ def tile_list_gatedsides_twotab_further_plain_kernel(
             copy(t[:].rearrange("p (t m) -> p m t", t=PACK), src[:].rearrange("p (m t) -> p m t", t=PACK))
             return t
 
-        def deal_slots(dealt, src, t0, t1):
-            nc.vector.tensor_copy(
-                dealt[:].rearrange("p (t m) -> p m t", t=PACK)[:, :, t0:t1],
-                src[:].rearrange("p (m t) -> p m t", t=PACK)[:, :, t0:t1],
-            )
-
         def fp8_words(src):
             return src[0].rearrange("p n t -> p (n t)")
 
+        xo_s = zeroed_plane(Z, "xo_s")
+        w2_s = zeroed_plane(R, "w2_s")
         xt_s = zeroed_plane(T, "xt_s")
+        w_s = zeroed_plane(R, "w_s")
         ws_s = zeroed_plane(N, "ws_s")
         wb_s = zeroed_plane(N, "wb_s")
-        w2_s = zeroed_plane(R, "w2_s")
-        xo_s = zeroed_plane(Z, "xo_s")
-        w_s = zeroed_plane(R, "w_s")
 
-        xo_w = load_words(xo_words[0], Z, U16, "xo_w", nc.scalar)
-        w2_w = load_words(fp8_words(w2_words), R, U32, "w2_w", nc.scalar)
-        w_w = load_words(w_words[0], R, U16, "w_w", nc.scalar)
-        xt_w = load_words(fp8_words(xt_words), T, U32, "xt_w", nc.scalar)
         w2_rows = load_scale_rows(w2_scales, "w2_rows")
-        xo_rows = load_scale_rows(xo_scales, "xo_rows")
         list2 = load_list(offs2, "list2")
-        w_rows = load_scale_rows(w_scales, "w_rows")
+        xo_w = load_words(xo_words[0], Z, U16, "xo_w")
+        load_plane(xo_s, xo_scales)
+        w2_w = load_words(fp8_words(w2_words), R, U32, "w2_w")
+        w_w = load_words(w_words[0], R, U16, "w_w")
+        xt_w = load_words(fp8_words(xt_words), T, U32, "xt_w")
         list6 = load_list(offs6, "list6")
         sh_c = load_column(sh, "sh_c")
         bh_c = load_column(bh, "bh_c")
-        list1 = load_list(offs, "list1")
-        load_plane(xt_s, xt_scales)
         list5 = load_list(offs5, "list5")
         sb_c = load_column(sb, "sb_c")
+        list1 = load_list(offs, "list1")
+        load_plane(xt_s, xt_scales)
+        load_plane(w_s, w_scales)
         list4 = load_list(offs4, "list4")
         sg_c = load_column(sg, "sg_c")
         bg_c = load_column(bg, "bg_c")
@@ -181,7 +175,7 @@ def tile_list_gatedsides_twotab_further_plain_kernel(
                 banks.append(acc)
             return banks
 
-        def finish(side, banks, codes, scales, d0, copiers, queues, tags):
+        def finish(side, banks, codes, scales, d0, copiers, queues):
             for n in range(N // P):
                 cols = slice(n * P, (n + 1) * P)
                 nc.tensor.matmul_mx(
@@ -189,29 +183,24 @@ def tile_list_gatedsides_twotab_further_plain_kernel(
                     rhs=codes[:].bitcast(E4M3), rhs_scale=scales[:], start=False, stop=True,
                 )
             for n in range(N // P):
-                res = tile([P, O], F32, "%s_res%d" % (side, n), tags[n])
+                res = tile([P, O], F32, "%s_res%d" % (side, n))
                 copiers[n](res[:], banks[n][:])
                 queues[n].dma_start(out[n * P : (n + 1) * P, d0 : d0 + O], res[:])
 
         vcopy, scopy = nc.vector.tensor_copy, nc.scalar.copy
 
         spread(w2_s, w2_rows)
-        spread(xo_s, xo_rows)
-        w2_sd = tile([P, R], U8, "w2_sd")
-        deal_slots(w2_sd, w2_s, 0, 1)
         xo_gw = gather(xo_w, list2, U16, "xo_gw")
+        w2_sd = deal(vcopy, w2_s, U8, "w2_sd")
         xo_gs = gather(xo_s, list2, U8, "xo_gs")
-        deal_slots(w2_sd, w2_s, 1, PACK)
         w2_wd = deal(scopy, w2_w, U32, "w2_wd")
         w_wd = deal(scopy, w_w, U16, "w_wd")
         b_banks = first_stage("b", 0, w2_wd, w2_sd, E5M2, xo_gw, xo_gs, E2M1)
 
-        spread(w_s, w_rows)
-        w_sd = tile([P, R], U8, "w_sd")
-        deal_slots(w_sd, w_s, 0, PACK)
         xt_gw = gather(xt_w, list1, U32, "xt_gw")
         xt_gs = gather(xt_s, list1, U8, "xt_gs")
-        b_gates, b_values = looks("b", b_banks, [scopy, scopy, scopy, vcopy], list6, sh_c, bh_c, list5, sb_c)
+        w_sd = deal(vcopy, w_s, U8, "w_sd")
+        b_gates, b_values = looks("b", b_banks, [scopy, vcopy, vcopy, vcopy], list6, sh_c, bh_c, list5, sb_c)
         a_banks = first_stage("a", 4, w_wd, w_sd, E2M1, xt_gw, xt_gs, E4M3)
         a_gates, a_values = looks("a", a_banks, [vcopy] * 4, list4, sg_c, bg_c, list3, sa_c)
 
@@ -219,7 +208,7 @@ def tile_list_gatedsides_twotab_further_plain_kernel(
         x7_w = gather(xt_w, list7, U32, "x7_w", "xt_gw")
         x7_s = gather(xt_s, list7, U8, "x7_s", "xt_gs")
         b_out = short_way("b", 4, O)
-        finish("b", b_out, b_codes, b_scales, O, [scopy, scopy], [nc.sync, nc.sync], ["a_rows2", "a_rows3"])
+        finish("b", b_out, b_codes, b_scales, O, [vcopy, vcopy], [nc.sync, nc.sync])
         a_out = short_way("a", 6, 0)
         a_codes, a_scales = hidden("a", a_gates, a_values)
-        finish("a", a_out, a_codes, a_scales, 0, [vcopy, scopy], [nc.sync, nc.scalar], [None, None])
+        finish("a", a_out, a_codes, a_scales, 0, [vcopy, scopy], [nc.sync, nc.scalar])

from contextlib import ExitStack

import concourse.mybir as mybir

K, T, J, R, Z, O, D, N = 512, 1024, 256, 512, 1024, 128, 256, 256
FLOPS = 2 * (K * R * J + K * R * J + R * N * D + K * N * D)

F32 = mybir.dt.float32
BF16 = mybir.dt.bfloat16
I32 = mybir.dt.int32
U32 = mybir.dt.uint32
U16 = mybir.dt.uint16
U8 = mybir.dt.uint8
E4M3 = mybir.dt.float8_e4m3fn_x4
E5M2 = mybir.dt.float8_e5m2_x4
E2M1 = mybir.dt.float4_e2m1fn_x4
ACT = mybir.ActivationFunctionType
MULT = mybir.AluOpType.mult

P = 128
PACK = 4
QUADS = 4
QUAD = 32


def tile_list_gatedsides_twotab_further_plain_kernel(
    tc, xt_words, xt_scales, xo_words, xo_scales, w_words, w_scales, w2_words, w2_scales,
    sa, sb, sg, bg, sh, bh, wb_words, wb_scales, ws_words, ws_scales,
    offs, offs2, offs3, offs4, offs5, offs6, offs7, out,
):
    nc = tc.nc
    with ExitStack() as ctx:
        keep = ctx.enter_context(tc.tile_pool(name="keep", bufs=1))
        psum = ctx.enter_context(tc.psum_pool(name="psum", bufs=1))

        def tile(shape, dtype, name, tag=None):
            return keep.tile(shape, dtype, name=name, tag=tag or name, align_bytes=64)

        def load_list(src, name):
            t = tile(list(src.shape), U16, name)
            nc.sync.dma_start(t[:], src)
            return t

        def load_words(src, cols, dtype, name):
            t = tile([P, cols], dtype, name)
            nc.sync.dma_start(t[:].bitcast(I32), src.bitcast(I32))
            return t

        def load_scale_rows(src, name):
            cols = src.shape[2]
            t = tile([PACK, QUADS, cols // 4], I32, name)
            nc.sync.dma_start(t[:], src[0].rearrange("(q r) n -> r q n", r=PACK).bitcast(I32))
            return t

        def load_column(src, name):
            t = tile([P, PACK], F32, name)
            nc.sync.dma_start(t[:], src.rearrange("(p t) o -> p (t o)", t=PACK))
            return t

        def zeroed_plane(cols, name):
            t = tile([P, cols], U8, name)
            nc.vector.memset(t[:].bitcast(I32), 0)
            return t

        def load_plane(plane, src):
            for q in range(QUADS):
                nc.sync.dma_start(
                    plane[QUAD * q : QUAD * q + PACK, :].bitcast(I32), src[0, PACK * q : PACK * (q + 1), :].bitcast(I32)
                )

        def spread(plane, rows):
            for q in range(QUADS):
                nc.vector.tensor_copy(plane[QUAD * q : QUAD * q + PACK, :].bitcast(I32), rows[:, q, :])

        def gather(window, offsets, dtype, name, tag=None):
            t = tile([P, 16 * offsets.shape[1]], dtype, name, tag)
            nc.vector.tensor_copy(t[:], window[:].indirect(offsets[:]))
            return t

        def deal(copy, src, dtype, name):
            t = tile([P, R], dtype, name)
            copy(t[:].rearrange("p (t m) -> p m t", t=PACK), src[:].rearrange("p (m t) -> p m t", t=PACK))
            return t

        def fp8_words(src):
            return src[0].rearrange("p n t -> p (n t)")

        xo_s = zeroed_plane(Z, "xo_s")
        w2_s = zeroed_plane(R, "w2_s")
        xt_s = zeroed_plane(T, "xt_s")
        w_s = zeroed_plane(R, "w_s")
        ws_s = zeroed_plane(N, "ws_s")
        wb_s = zeroed_plane(N, "wb_s")

        w2_rows = load_scale_rows(w2_scales, "w2_rows")
        list2 = load_list(offs2, "list2")
        xo_w = load_words(xo_words[0], Z, U16, "xo_w")
        load_plane(xo_s, xo_scales)
        w2_w = load_words(fp8_words(w2_words), R, U32, "w2_w")
        w_w = load_words(w_words[0], R, U16, "w_w")
        xt_w = load_words(fp8_words(xt_words), T, U32, "xt_w")
        list6 = load_list(offs6, "list6")
        sh_c = load_column(sh, "sh_c")
        bh_c = load_column(bh, "bh_c")
        list5 = load_list(offs5, "list5")
        sb_c = load_column(sb, "sb_c")
        list1 = load_list(offs, "list1")
        load_plane(xt_s, xt_scales)
        load_plane(w_s, w_scales)
        list4 = load_list(offs4, "list4")
        sg_c = load_column(sg, "sg_c")
        bg_c = load_column(bg, "bg_c")
        list3 = load_list(offs3, "list3")
        sa_c = load_column(sa, "sa_c")
        list7 = load_list(offs7, "list7")
        ws_w = load_words(fp8_words(ws_words), N, U32, "ws_w")
        wb_w = load_words(fp8_words(wb_words), N, U32, "wb_w")
        load_plane(ws_s, ws_scales)
        load_plane(wb_s, wb_scales)

        warm_in = tile([P, 1], F32, "warm_in")
        warm_out = tile([P, 1], F32, "warm_out")
        nc.vector.memset(warm_in[:], 0.0)
        nc.scalar.activation(out=warm_out[:], in_=warm_in[:], func=ACT.Sigmoid)
        def first_stage(side, bank0, lhs_w, lhs_s, lhs_fmt, rhs_w, rhs_s, rhs_fmt):
            banks = []
            for t in range(PACK):
                cols = slice(t * P, (t + 1) * P)
                acc = psum.tile([P, J], F32, name="%s_acc%d" % (side, t), tag="bank%d" % (bank0 + t))
                nc.tensor.matmul_mx(
                    out=acc[:], lhsT=lhs_w[:, cols].bitcast(lhs_fmt), lhsT_scale=lhs_s[:, cols],
                    rhs=rhs_w[:].bitcast(rhs_fmt), rhs_scale=rhs_s[:], start=True, stop=True,
                )
                banks.append(acc)
            return banks

        def looks(side, banks, copiers, gate_list, slope, offset, value_list, weight):
            gates = tile([P, PACK, O], F32, side + "_gates")
            values = tile([P, PACK, O], F32, side + "_values")
            for t in range(PACK):
                rows = tile([P, J], F32, "%s_rows%d" % (side, t))
                copiers[t](rows[:], banks[t][:])
                nc.scalar.activation(
                    out=gates[:, t, :], in_=rows[:].indirect(gate_list[:]), func=ACT.Sigmoid,
                    bias=offset[:, t : t + 1], scale=slope[:, t : t + 1],
                )
                nc.scalar.activation(
                    out=values[:, t, :], in_=rows[:].indirect(value_list[:]), func=ACT.Copy,
                    scale=weight[:, t : t + 1],
                )
            return gates, values

        def hidden(side, gates, values, tag=None):
            hid = tile([P, O * PACK], BF16, side + "_hid", tag)
            nc.vector.tensor_tensor(
                hid[:].rearrange("p (c i t) -> p c t i", i=4, t=PACK),
                values[:].rearrange("p t (c i) -> p c t i", i=4),
                gates[:].rearrange("p t (c i) -> p c t i", i=4),
                MULT,
            )
            codes = tile([P, O], U32, side + "_codes")
            scales = tile([P, O], U8, side + "_scales")
            nc.vector.quantize_mx(out=codes[:].bitcast(E4M3), scales=scales[:], in_=hid[:])
            return codes, scales

        def short_way(side, bank0, d0):
            banks = []
            for n in range(N // P):
                cols = slice(n * P, (n + 1) * P)
                acc = psum.tile([P, O], F32, name="%s_out%d" % (side, n), tag="bank%d" % (bank0 + n))
                nc.tensor.matmul_mx(
                    out=acc[:], lhsT=ws_w[:, cols].bitcast(E5M2), lhsT_scale=ws_s[:, cols],
                    rhs=x7_w[:, d0 : d0 + O].bitcast(E4M3), rhs_scale=x7_s[:, d0 : d0 + O], start=True, stop=False,
                )
                banks.append(acc)
            return banks

        def finish(side, banks, codes, scales, d0, copiers, queues):
            for n in range(N // P):
                cols = slice(n * P, (n + 1) * P)
                nc.tensor.matmul_mx(
                    out=banks[n][:], lhsT=wb_w[:, cols].bitcast(E5M2), lhsT_scale=wb_s[:, cols],
                    rhs=codes[:].bitcast(E4M3), rhs_scale=scales[:], start=False, stop=True,
                )
            for n in range(N // P):
                res = tile([P, O], F32, "%s_res%d" % (side, n))
                copiers[n](res[:], banks[n][:])
                queues[n].dma_start(out[n * P : (n + 1) * P, d0 : d0 + O], res[:])

        vcopy, scopy = nc.vector.tensor_copy, nc.scalar.copy

        spread(w2_s, w2_rows)
        xo_gw = gather(xo_w, list2, U16, "xo_gw")
        w2_sd = deal(vcopy, w2_s, U8, "w2_sd")
        xo_gs = gather(xo_s, list2, U8, "xo_gs")
        w2_wd = deal(scopy, w2_w, U32, "w2_wd")
        w_wd = deal(scopy, w_w, U16, "w_wd")
        b_banks = first_stage("b", 0, w2_wd, w2_sd, E5M2, xo_gw, xo_gs, E2M1)

        xt_gw = gather(xt_w, list1, U32, "xt_gw")
        xt_gs = gather(xt_s, list1, U8, "xt_gs")
        w_sd = deal(vcopy, w_s, U8, "w_sd")
        b_gates, b_values = looks("b", b_banks, [scopy, vcopy, vcopy, vcopy], list6, sh_c, bh_c, list5, sb_c)
        a_banks = first_stage("a", 4, w_wd, w_sd, E2M1, xt_gw, xt_gs, E4M3)
        a_gates, a_values = looks("a", a_banks, [vcopy] * 4, list4, sg_c, bg_c, list3, sa_c)

        b_codes, b_scales = hidden("b", b_gates, b_values, "w_wd")
        x7_w = gather(xt_w, list7, U32, "x7_w", "xt_gw")
        x7_s = gather(xt_s, list7, U8, "x7_s", "xt_gs")
        b_out = short_way("b", 4, O)
        finish("b", b_out, b_codes, b_scales, O, [vcopy, vcopy], [nc.sync, nc.sync])
        a_out = short_way("a", 6, 0)
        a_codes, a_scales = hidden("a", a_gates, a_values)
        finish("a", a_out, a_codes, a_scales, 0, [vcopy, scopy], [nc.sync, nc.scalar])
